import numpy as np, ml_dtypes
CORES = [19,147,275,403]
N = 4
S, B = 8, 128
def setup_inputs(rng):
    a = (rng.standard_normal((128, 128), dtype=np.float32) / 8).astype(ml_dtypes.bfloat16)
    return {"x": (rng.standard_normal((N, 128, S * B), dtype=np.float32) / 2).astype(ml_dtypes.bfloat16), "a": np.broadcast_to(a, (N, 128, 128)).copy()}
def reference(x, a):
    X, A = x.astype(np.float64), a.astype(np.float64)
    y = np.zeros((N, 128, S * B)); h = np.zeros((128, B))
    for r in range(N):
        for s in range(S):
            h = np.tanh(A[r].T @ h + X[r][:, B * s:B * s + B])
            y[r][:, B * s:B * s + B] = h
    return {"y": y.astype(ml_dtypes.bfloat16)}

@@ -1,0 +1,165 @@
+from concourse.mybir import AluOpType, ActivationFunctionType
+
+S, B = 8, 128
+HB = B // 2
+STREAM = [(0, 1), (1, 4), (4, 6), (6, 8)]
+WHOLE = [(0, 8)]
+TAIL = [(0, 4), (4, 6), (6, 7), (7, 8)]
+BLOCKS = [[0, 1], [0, 1], [2], [2, 3]]
+X_TO = [1, 0, 3, None]
+
+SCRATCH = {
+    "a_sb": ("sbuf", [128, 128], "bfloat16"),
+    "ident": ("sbuf", [128, 128], "bfloat16"),
+    "xs": ("sbuf", [128, S * B], "bfloat16"),
+    "xr": ("sbuf", [128, S * B], "bfloat16"),
+    "hin": ("sbuf", [128, B], "bfloat16"),
+    "ys": ("sbuf", [128, 2 * S * B], "bfloat16"),
+    "z0": ("sbuf", [128, HB], "float32"),
+    "z1": ("sbuf", [128, HB], "float32"),
+}
+for _i in range(8):
+    SCRATCH["ps%d" % _i] = ("psum", [128, 512], "float32")
+
+SEMAPHORES = (["ones", "id", "la", "rh", "mA", "mB", "vA", "vB", "tA", "tB", "sx", "sh", "st"]
+              + ["lx%d" % i for i in range(len(STREAM))] + ["rx%d" % i for i in range(len(STREAM))])
+
+
+def _pieces(r):
+    return STREAM if BLOCKS[r][0] == 0 else WHOLE
+
+
+def _engines(mask):
+    return bin(mask).count("1")
+
+
+def rank_program(g, core, T, topo):
+    rank = T.rank_of(core)
+    if rank is None:
+        return
+    cores, sem = T.cores, T.sem
+    blocks = BLOCKS[rank]
+    first = blocks[0] == 0
+    nj = S * len(blocks)
+    j0 = S * blocks.index(rank)
+    holders = [r for r in range(len(cores)) if BLOCKS[r][-1] == 1]
+    takers = [r for r in range(len(cores)) if BLOCKS[r][0] == 2]
+    h_src = {d: [s for s in holders if topo.may_write(cores[s], cores[d])][0] for d in takers}
+    h_to = [d for d in takers if h_src[d] == rank]
+
+    xof = {}
+    for bi, b in enumerate(blocks):
+        own = b == rank
+        for i, (lo, hi) in enumerate(_pieces(b)):
+            for s in range(lo, hi):
+                xof[S * bi + s] = (T.xs if own else T.xr, s, sem[("lx%d" if own else "rx%d") % i],
+                                   16 if own else _engines(topo.mask(cores[b], core)), (bi, i))
+    if first:
+        prepared = [j for j in range(j0, j0 + S) if j > 0][:3]
+        pbank = {j: 2 + 2 * k for k, j in enumerate(prepared)}
+    else:
+        prepared = list(range(4))
+        pbank = {j: 2 * k for k, j in enumerate(prepared)}
+    kind = {j: "D" if first and j == 0 else "P" if j in pbank else "V" for j in range(nj)}
+
+    def psum(j, c):
+        return T["ps%d" % ((pbank[j] if kind[j] == "P" else 0) + c)][:, 0:HB]
+
+    def xcols(j, c):
+        return xof[j][0][:, xof[j][1] * B + c * HB: xof[j][1] * B + (c + 1) * HB]
+
+    def hcols(j, c):
+        return T.ys[:, j * B + c * HB: j * B + (c + 1) * HB]
+
+    def x_ready(q, j, seen):
+        if xof[j][4] not in seen:
+            seen.add(xof[j][4])
+            q.wait_ge(xof[j][2], xof[j][3])
+
+    msem, vsem, tsem, zbuf = (sem.mA, sem.mB), (sem.vA, sem.vB), (sem.tA, sem.tB), (T.z0, T.z1)
+    mcount = {j: len([k for k in range(j + 1) if kind[k] != "D"]) for j in range(nj)}
+    vcount = {j: len([k for k in range(j + 1) if kind[k] == "V"]) for j in range(nj)}
+
+    mine = _pieces(rank)
+    for i, (lo, hi) in enumerate(mine):
+        g.sync.dma_start(T.xs[:, lo * B:hi * B], T.x[:, lo * B:hi * B]).then_inc(sem["lx%d" % i], 16)
+    g.scalar.dma_start(T.a_sb[:], T.a[:]).then_inc(sem.la, 16)
+    g.vector.memset(T.ident[:], 1.0).then_inc(sem.ones, 1)
+    g.wait_ge(sem.ones, 1)
+    g.affine_select(T.ident[:], T.ident[:], [[-1, 128]], AluOpType.is_equal, 0.0, 0, 1).then_inc(sem.id, 1)
+
+    tq, seen = g.tensor, set()
+    tq.wait_ge(sem.id, 1)
+    for j in prepared:
+        x_ready(tq, j, seen)
+        for c in (0, 1):
+            tq.matmul(psum(j, c), T.ident[:], xcols(j, c), True, False)
+    tq.wait_ge(sem.la, 16)
+    if not first:
+        tq.wait_ge(sem.rh, _engines(topo.mask(cores[h_src[rank]], core)))
+    for j in range(nj):
+        for c in (0, 1):
+            if kind[j] == "D":
+                continue
+            if j > 0:
+                tq.wait_ge(tsem[c], j)
+            prev = hcols(j - 1, c) if j > 0 else T.hin[:, c * HB:(c + 1) * HB]
+            tq.matmul(psum(j, c), T.a_sb[:], prev, kind[j] == "V", True).then_inc(msem[c], 1)
+
+    vq, seen = g.vector, set()
+    for j in range(nj):
+        if kind[j] == "V":
+            x_ready(vq, j, seen)
+            for c in (0, 1):
+                vq.wait_ge(msem[c], mcount[j])
+                vq.tensor_tensor(zbuf[c][:], psum(j, c), xcols(j, c), AluOpType.add).then_inc(vsem[c], 1)
+
+    sq, seen = g.scalar, set()
+    for j in range(nj):
+        for c in (0, 1):
+            if kind[j] == "D":
+                x_ready(sq, j, seen)
+                src = xcols(j, c)
+            elif kind[j] == "P":
+                sq.wait_ge(msem[c], mcount[j])
+                src = psum(j, c)
+            else:
+                sq.wait_ge(vsem[c], vcount[j])
+                src = zbuf[c][:]
+            sq.activation(hcols(j, c), src, ActivationFunctionType.Tanh).then_inc(tsem[c], 1)
+
+    sent = 0
+    if X_TO[rank] is not None:
+        dst = cores[X_TO[rank]]
+        rid, pid = topo.addr(dst, core)
+        m = topo.mask(core, dst)
+        for i, (lo, hi) in enumerate(mine):
+            g.wait_ge(sem["lx%d" % i], 16)
+            g.remote_dma(out_ap=T.xr[:, lo * B:hi * B], in_ap=T.xs[:, lo * B:hi * B], remote_sem=sem["rx%d" % i],
+                         local_sem=sem.sx, pid=pid, routing_id=rid, dma_engine_mask=m)
+            sent += _engines(m)
+    hsent = 0
+    for d in h_to:
+        dst = cores[d]
+        rid, pid = topo.addr(dst, core)
+        m = topo.mask(core, dst)
+        g.wait_ge(sem.tA, nj)
+        g.wait_ge(sem.tB, nj)
+        g.remote_dma(out_ap=T.hin[:], in_ap=T.ys[:, (nj - 1) * B:nj * B], remote_sem=sem.rh, local_sem=sem.sh,
+                     pid=pid, routing_id=rid, dma_engine_mask=m)
+        hsent += _engines(m)
+    if sent:
+        g.wait_ge(sem.sx, sent)
+    if hsent:
+        g.wait_ge(sem.sh, hsent)
+
+    if hsent:
+        g.sync.wait_ge(sem.sh, hsent)
+        parts = WHOLE
+    else:
+        parts = TAIL
+    for lo, hi in parts:
+        g.sync.wait_ge(sem.tA, j0 + hi)
+        g.sync.wait_ge(sem.tB, j0 + hi)
+        g.sync.dma_start(T.y[:, lo * B:hi * B], T.ys[:, (j0 + lo) * B:(j0 + hi) * B]).then_inc(sem.st, 16)
+    g.sync.wait_ge(sem.st, 16 * len(parts))

@@ -2,11 +2,13 @@ from concourse.mybir import AluOpType, ActivationFunctionType
 
 S, B = 8, 128
 HB = B // 2
-STREAM = [(0, 1), (1, 4), (4, 6), (6, 8)]
-WHOLE = [(0, 8)]
+STREAM = [(0, 1, (0, 8)), (1, 4, (0, 8)), (4, 6, (0, 8)), (6, 8, (0, 8))]
+WHOLE = [(0, 8, (0, 8))]
+H_ENG = (0, 8)
 TAIL = [(0, 4), (4, 6), (6, 7), (7, 8)]
 BLOCKS = [[0, 1], [0, 1], [2], [2, 3]]
 X_TO = [1, 0, 3, None]
+AHEAD = 4
 
 SCRATCH = {
     "a_sb": ("sbuf", [128, 128], "bfloat16"),
@@ -15,13 +17,11 @@ SCRATCH = {
     "xr": ("sbuf", [128, S * B], "bfloat16"),
     "hin": ("sbuf", [128, B], "bfloat16"),
     "ys": ("sbuf", [128, 2 * S * B], "bfloat16"),
-    "z0": ("sbuf", [128, HB], "float32"),
-    "z1": ("sbuf", [128, HB], "float32"),
 }
-for _i in range(8):
+for _i in range(2 * AHEAD):
     SCRATCH["ps%d" % _i] = ("psum", [128, 512], "float32")
 
-SEMAPHORES = (["ones", "id", "la", "rh", "mA", "mB", "vA", "vB", "tA", "tB", "sx", "sh", "st"]
+SEMAPHORES = (["ones", "id", "la", "rh", "mA", "mB", "tA", "tB", "sx", "sh", "st"]
               + ["lx%d" % i for i in range(len(STREAM))] + ["rx%d" % i for i in range(len(STREAM))])
 
 
@@ -29,8 +29,9 @@ def _pieces(r):
     return STREAM if BLOCKS[r][0] == 0 else WHOLE
 
 
-def _engines(mask):
-    return bin(mask).count("1")
+def _sub(mask, eng):
+    bits = [b for b in range(16) if (mask >> b) & 1][eng[0]:eng[0] + eng[1]]
+    return sum(1 << b for b in bits)
 
 
 def rank_program(g, core, T, topo):
@@ -42,6 +43,7 @@ def rank_program(g, core, T, topo):
     first = blocks[0] == 0
     nj = S * len(blocks)
     j0 = S * blocks.index(rank)
+    jp = 1 if first else 0
     holders = [r for r in range(len(cores)) if BLOCKS[r][-1] == 1]
     takers = [r for r in range(len(cores)) if BLOCKS[r][0] == 2]
     h_src = {d: [s for s in holders if topo.may_write(cores[s], cores[d])][0] for d in takers}
@@ -50,20 +52,13 @@ def rank_program(g, core, T, topo):
     xof = {}
     for bi, b in enumerate(blocks):
         own = b == rank
-        for i, (lo, hi) in enumerate(_pieces(b)):
+        for i, (lo, hi, eng) in enumerate(_pieces(b)):
             for s in range(lo, hi):
                 xof[S * bi + s] = (T.xs if own else T.xr, s, sem[("lx%d" if own else "rx%d") % i],
-                                   16 if own else _engines(topo.mask(cores[b], core)), (bi, i))
-    if first:
-        prepared = [j for j in range(j0, j0 + S) if j > 0][:3]
-        pbank = {j: 2 + 2 * k for k, j in enumerate(prepared)}
-    else:
-        prepared = list(range(4))
-        pbank = {j: 2 * k for k, j in enumerate(prepared)}
-    kind = {j: "D" if first and j == 0 else "P" if j in pbank else "V" for j in range(nj)}
+                                   16 if own else eng[1], (bi, i), own or not first)
 
     def psum(j, c):
-        return T["ps%d" % ((pbank[j] if kind[j] == "P" else 0) + c)][:, 0:HB]
+        return T["ps%d" % (2 * (j % AHEAD) + c)][:, 0:HB]
 
     def xcols(j, c):
         return xof[j][0][:, xof[j][1] * B + c * HB: xof[j][1] * B + (c + 1) * HB]
@@ -76,78 +71,69 @@ def rank_program(g, core, T, topo):
             seen.add(xof[j][4])
             q.wait_ge(xof[j][2], xof[j][3])
 
-    msem, vsem, tsem, zbuf = (sem.mA, sem.mB), (sem.vA, sem.vB), (sem.tA, sem.tB), (T.z0, T.z1)
-    mcount = {j: len([k for k in range(j + 1) if kind[k] != "D"]) for j in range(nj)}
-    vcount = {j: len([k for k in range(j + 1) if kind[k] == "V"]) for j in range(nj)}
+    msem, tsem = (sem.mA, sem.mB), (sem.tA, sem.tB)
 
     mine = _pieces(rank)
-    for i, (lo, hi) in enumerate(mine):
+    for i, (lo, hi, eng) in enumerate(mine):
         g.sync.dma_start(T.xs[:, lo * B:hi * B], T.x[:, lo * B:hi * B]).then_inc(sem["lx%d" % i], 16)
     g.scalar.dma_start(T.a_sb[:], T.a[:]).then_inc(sem.la, 16)
     g.vector.memset(T.ident[:], 1.0).then_inc(sem.ones, 1)
     g.wait_ge(sem.ones, 1)
     g.affine_select(T.ident[:], T.ident[:], [[-1, 128]], AluOpType.is_equal, 0.0, 0, 1).then_inc(sem.id, 1)
 
-    tq, seen = g.tensor, set()
+    tq, seen, put = g.tensor, set(), set()
+
+    def prepare(upto, must):
+        for k in range(jp, min(upto, nj - 1) + 1):
+            if k not in put and (k == must or xof[k][5] or xof[k][4] in seen):
+                x_ready(tq, k, seen)
+                put.add(k)
+                for c in (0, 1):
+                    tq.matmul(psum(k, c), T.ident[:], xcols(k, c), True, False)
+
     tq.wait_ge(sem.id, 1)
-    for j in prepared:
-        x_ready(tq, j, seen)
-        for c in (0, 1):
-            tq.matmul(psum(j, c), T.ident[:], xcols(j, c), True, False)
+    prepare(jp + AHEAD - 1, jp)
     tq.wait_ge(sem.la, 16)
     if not first:
-        tq.wait_ge(sem.rh, _engines(topo.mask(cores[h_src[rank]], core)))
-    for j in range(nj):
+        tq.wait_ge(sem.rh, H_ENG[1])
+    for j in range(jp, nj):
         for c in (0, 1):
-            if kind[j] == "D":
-                continue
             if j > 0:
                 tq.wait_ge(tsem[c], j)
             prev = hcols(j - 1, c) if j > 0 else T.hin[:, c * HB:(c + 1) * HB]
-            tq.matmul(psum(j, c), T.a_sb[:], prev, kind[j] == "V", True).then_inc(msem[c], 1)
+            tq.matmul(psum(j, c), T.a_sb[:], prev, False, True).then_inc(msem[c], 1)
+        prepare(j + AHEAD - 1, j + 1)
 
-    vq, seen = g.vector, set()
-    for j in range(nj):
-        if kind[j] == "V":
-            x_ready(vq, j, seen)
-            for c in (0, 1):
-                vq.wait_ge(msem[c], mcount[j])
-                vq.tensor_tensor(zbuf[c][:], psum(j, c), xcols(j, c), AluOpType.add).then_inc(vsem[c], 1)
-
-    sq, seen = g.scalar, set()
+    sq = g.scalar
     for j in range(nj):
         for c in (0, 1):
-            if kind[j] == "D":
-                x_ready(sq, j, seen)
+            if j < jp:
+                if c == 0:
+                    sq.wait_ge(xof[j][2], xof[j][3])
                 src = xcols(j, c)
-            elif kind[j] == "P":
-                sq.wait_ge(msem[c], mcount[j])
-                src = psum(j, c)
             else:
-                sq.wait_ge(vsem[c], vcount[j])
-                src = zbuf[c][:]
+                sq.wait_ge(msem[c], j - jp + 1)
+                src = psum(j, c)
             sq.activation(hcols(j, c), src, ActivationFunctionType.Tanh).then_inc(tsem[c], 1)
 
     sent = 0
     if X_TO[rank] is not None:
         dst = cores[X_TO[rank]]
         rid, pid = topo.addr(dst, core)
-        m = topo.mask(core, dst)
-        for i, (lo, hi) in enumerate(mine):
+        for i, (lo, hi, eng) in enumerate(mine):
             g.wait_ge(sem["lx%d" % i], 16)
             g.remote_dma(out_ap=T.xr[:, lo * B:hi * B], in_ap=T.xs[:, lo * B:hi * B], remote_sem=sem["rx%d" % i],
-                         local_sem=sem.sx, pid=pid, routing_id=rid, dma_engine_mask=m)
-            sent += _engines(m)
+                         local_sem=sem.sx, pid=pid, routing_id=rid, dma_engine_mask=_sub(topo.mask(core, dst), eng))
+            sent += eng[1]
     hsent = 0
     for d in h_to:
         dst = cores[d]
         rid, pid = topo.addr(dst, core)
-        m = topo.mask(core, dst)
         g.wait_ge(sem.tA, nj)
         g.wait_ge(sem.tB, nj)
         g.remote_dma(out_ap=T.hin[:], in_ap=T.ys[:, (nj - 1) * B:nj * B], remote_sem=sem.rh, local_sem=sem.sh,
-                     pid=pid, routing_id=rid, dma_engine_mask=m)
-        hsent += _engines(m)
+                     pid=pid, routing_id=rid, dma_engine_mask=_sub(topo.mask(core, dst), H_ENG))
+        hsent += H_ENG[1]
     if sent:
         g.wait_ge(sem.sx, sent)
     if hsent:
@@ -158,7 +144,8 @@ def rank_program(g, core, T, topo):
         parts = WHOLE
     else:
         parts = TAIL
-    for lo, hi in parts:
+    for part in parts:
+        lo, hi = part[0], part[1]
         g.sync.wait_ge(sem.tA, j0 + hi)
         g.sync.wait_ge(sem.tB, j0 + hi)
         g.sync.dma_start(T.y[:, lo * B:hi * B], T.ys[:, (j0 + lo) * B:(j0 + hi) * B]).then_inc(sem.st, 16)

@@ -1,14 +1,15 @@
 from concourse.mybir import AluOpType, ActivationFunctionType
 
 S, B = 8, 128
-HB = B // 2
-STREAM = [(0, 1, (0, 8)), (1, 4, (0, 8)), (4, 6, (0, 8)), (6, 8, (0, 8))]
+NC = 4
+HB = B // NC
+AHEAD = 8 // NC
+STREAM = [(0, 1, (0, 4)), (1, 4, (0, 4)), (4, 6, (0, 4)), (6, 8, (0, 4))]
 WHOLE = [(0, 8, (0, 8))]
-H_ENG = (0, 8)
+H_ENG = (0, 4)
 TAIL = [(0, 4), (4, 6), (6, 7), (7, 8)]
 BLOCKS = [[0, 1], [0, 1], [2], [2, 3]]
 X_TO = [1, 0, 3, None]
-AHEAD = 4
 
 SCRATCH = {
     "a_sb": ("sbuf", [128, 128], "bfloat16"),
@@ -18,10 +19,11 @@ SCRATCH = {
     "hin": ("sbuf", [128, B], "bfloat16"),
     "ys": ("sbuf", [128, 2 * S * B], "bfloat16"),
 }
-for _i in range(2 * AHEAD):
+for _i in range(NC * AHEAD):
     SCRATCH["ps%d" % _i] = ("psum", [128, 512], "float32")
 
-SEMAPHORES = (["ones", "id", "la", "rh", "mA", "mB", "tA", "tB", "sx", "sh", "st"]
+SEMAPHORES = (["ones", "id", "la", "rh", "sx", "sh", "st"]
+              + ["m%d" % c for c in range(NC)] + ["t%d" % c for c in range(NC)]
               + ["lx%d" % i for i in range(len(STREAM))] + ["rx%d" % i for i in range(len(STREAM))])
 
 
@@ -58,7 +60,7 @@ def rank_program(g, core, T, topo):
                                    16 if own else eng[1], (bi, i), own or not first)
 
     def psum(j, c):
-        return T["ps%d" % (2 * (j % AHEAD) + c)][:, 0:HB]
+        return T["ps%d" % (NC * (j % AHEAD) + c)][:, 0:HB]
 
     def xcols(j, c):
         return xof[j][0][:, xof[j][1] * B + c * HB: xof[j][1] * B + (c + 1) * HB]
@@ -71,7 +73,12 @@ def rank_program(g, core, T, topo):
             seen.add(xof[j][4])
             q.wait_ge(xof[j][2], xof[j][3])
 
-    msem, tsem = (sem.mA, sem.mB), (sem.tA, sem.tB)
+    msem = [sem["m%d" % c] for c in range(NC)]
+    tsem = [sem["t%d" % c] for c in range(NC)]
+
+    def done(q, n):
+        for c in range(NC):
+            q.wait_ge(tsem[c], n)
 
     mine = _pieces(rank)
     for i, (lo, hi, eng) in enumerate(mine):
@@ -88,7 +95,7 @@ def rank_program(g, core, T, topo):
             if k not in put and (k == must or xof[k][5] or xof[k][4] in seen):
                 x_ready(tq, k, seen)
                 put.add(k)
-                for c in (0, 1):
+                for c in range(NC):
                     tq.matmul(psum(k, c), T.ident[:], xcols(k, c), True, False)
 
     tq.wait_ge(sem.id, 1)
@@ -97,7 +104,7 @@ def rank_program(g, core, T, topo):
     if not first:
         tq.wait_ge(sem.rh, H_ENG[1])
     for j in range(jp, nj):
-        for c in (0, 1):
+        for c in range(NC):
             if j > 0:
                 tq.wait_ge(tsem[c], j)
             prev = hcols(j - 1, c) if j > 0 else T.hin[:, c * HB:(c + 1) * HB]
@@ -106,7 +113,7 @@ def rank_program(g, core, T, topo):
 
     sq = g.scalar
     for j in range(nj):
-        for c in (0, 1):
+        for c in range(NC):
             if j < jp:
                 if c == 0:
                     sq.wait_ge(xof[j][2], xof[j][3])
@@ -129,8 +136,7 @@ def rank_program(g, core, T, topo):
     for d in h_to:
         dst = cores[d]
         rid, pid = topo.addr(dst, core)
-        g.wait_ge(sem.tA, nj)
-        g.wait_ge(sem.tB, nj)
+        done(g, nj)
         g.remote_dma(out_ap=T.hin[:], in_ap=T.ys[:, (nj - 1) * B:nj * B], remote_sem=sem.rh, local_sem=sem.sh,
                      pid=pid, routing_id=rid, dma_engine_mask=_sub(topo.mask(core, dst), H_ENG))
         hsent += H_ENG[1]
@@ -146,7 +152,6 @@ def rank_program(g, core, T, topo):
         parts = TAIL
     for part in parts:
         lo, hi = part[0], part[1]
-        g.sync.wait_ge(sem.tA, j0 + hi)
-        g.sync.wait_ge(sem.tB, j0 + hi)
+        done(g.sync, j0 + hi)
         g.sync.dma_start(T.y[:, lo * B:hi * B], T.ys[:, (j0 + lo) * B:(j0 + hi) * B]).then_inc(sem.st, 16)
     g.sync.wait_ge(sem.st, 16 * len(parts))

@@ -7,6 +7,7 @@ AHEAD = 8 // NC
 STREAM = [(0, 1, (0, 4)), (1, 4, (0, 4)), (4, 6, (0, 4)), (6, 8, (0, 4))]
 WHOLE = [(0, 8, (0, 8))]
 H_ENG = (0, 4)
+H_PARTS = [(0, 1), (1, NC)]
 TAIL = [(0, 4), (4, 6), (6, 7), (7, 8)]
 BLOCKS = [[0, 1], [0, 1], [2], [2, 3]]
 X_TO = [1, 0, 3, None]
@@ -22,7 +23,7 @@ SCRATCH = {
 for _i in range(NC * AHEAD):
     SCRATCH["ps%d" % _i] = ("psum", [128, 512], "float32")
 
-SEMAPHORES = (["ones", "id", "la", "rh", "sx", "sh", "st"]
+SEMAPHORES = (["ones", "id", "la", "sx", "sh", "st"] + ["rh%d" % i for i in range(len(H_PARTS))]
               + ["m%d" % c for c in range(NC)] + ["t%d" % c for c in range(NC)]
               + ["lx%d" % i for i in range(len(STREAM))] + ["rx%d" % i for i in range(len(STREAM))])
 
@@ -76,8 +77,8 @@ def rank_program(g, core, T, topo):
     msem = [sem["m%d" % c] for c in range(NC)]
     tsem = [sem["t%d" % c] for c in range(NC)]
 
-    def done(q, n):
-        for c in range(NC):
+    def done(q, n, parts=(0, NC)):
+        for c in range(parts[0], parts[1]):
             q.wait_ge(tsem[c], n)
 
     mine = _pieces(rank)
@@ -101,12 +102,14 @@ def rank_program(g, core, T, topo):
     tq.wait_ge(sem.id, 1)
     prepare(jp + AHEAD - 1, jp)
     tq.wait_ge(sem.la, 16)
-    if not first:
-        tq.wait_ge(sem.rh, H_ENG[1])
     for j in range(jp, nj):
         for c in range(NC):
             if j > 0:
                 tq.wait_ge(tsem[c], j)
+            else:
+                for i, (lo, hi) in enumerate(H_PARTS):
+                    if c == lo:
+                        tq.wait_ge(sem["rh%d" % i], H_ENG[1])
             prev = hcols(j - 1, c) if j > 0 else T.hin[:, c * HB:(c + 1) * HB]
             tq.matmul(psum(j, c), T.a_sb[:], prev, False, True).then_inc(msem[c], 1)
         prepare(j + AHEAD - 1, j + 1)
@@ -136,10 +139,12 @@ def rank_program(g, core, T, topo):
     for d in h_to:
         dst = cores[d]
         rid, pid = topo.addr(dst, core)
-        done(g, nj)
-        g.remote_dma(out_ap=T.hin[:], in_ap=T.ys[:, (nj - 1) * B:nj * B], remote_sem=sem.rh, local_sem=sem.sh,
-                     pid=pid, routing_id=rid, dma_engine_mask=_sub(topo.mask(core, dst), H_ENG))
-        hsent += H_ENG[1]
+        for i, (lo, hi) in enumerate(H_PARTS):
+            done(g, nj, (lo, hi))
+            g.remote_dma(out_ap=T.hin[:, lo * HB:hi * HB], in_ap=T.ys[:, (nj - 1) * B + lo * HB:(nj - 1) * B + hi * HB],
+                         remote_sem=sem["rh%d" % i], local_sem=sem.sh, pid=pid, routing_id=rid,
+                         dma_engine_mask=_sub(topo.mask(core, dst), H_ENG))
+            hsent += H_ENG[1]
     if sent:
         g.wait_ge(sem.sx, sent)
     if hsent:

from concourse.mybir import AluOpType, ActivationFunctionType

S, B = 8, 128
NC = 4
HB = B // NC
AHEAD = 8 // NC
STREAM = [(0, 1, (0, 4)), (1, 4, (0, 4)), (4, 6, (0, 4)), (6, 8, (0, 4))]
WHOLE = [(0, 8, (0, 8))]
H_ENG = (0, 4)
H_PARTS = [(0, 1), (1, NC)]
TAIL = [(0, 4), (4, 6), (6, 7), (7, 8)]
BLOCKS = [[0, 1], [0, 1], [2], [2, 3]]
X_TO = [1, 0, 3, None]

SCRATCH = {
    "a_sb": ("sbuf", [128, 128], "bfloat16"),
    "ident": ("sbuf", [128, 128], "bfloat16"),
    "xs": ("sbuf", [128, S * B], "bfloat16"),
    "xr": ("sbuf", [128, S * B], "bfloat16"),
    "hin": ("sbuf", [128, B], "bfloat16"),
    "ys": ("sbuf", [128, 2 * S * B], "bfloat16"),
}
for _i in range(NC * AHEAD):
    SCRATCH["ps%d" % _i] = ("psum", [128, 512], "float32")

SEMAPHORES = (["ones", "id", "la", "sx", "sh", "st"] + ["rh%d" % i for i in range(len(H_PARTS))]
              + ["m%d" % c for c in range(NC)] + ["t%d" % c for c in range(NC)]
              + ["lx%d" % i for i in range(len(STREAM))] + ["rx%d" % i for i in range(len(STREAM))])


def _pieces(r):
    return STREAM if BLOCKS[r][0] == 0 else WHOLE


def _sub(mask, eng):
    bits = [b for b in range(16) if (mask >> b) & 1][eng[0]:eng[0] + eng[1]]
    return sum(1 << b for b in bits)


def rank_program(g, core, T, topo):
    rank = T.rank_of(core)
    if rank is None:
        return
    cores, sem = T.cores, T.sem
    blocks = BLOCKS[rank]
    first = blocks[0] == 0
    nj = S * len(blocks)
    j0 = S * blocks.index(rank)
    jp = 1 if first else 0
    holders = [r for r in range(len(cores)) if BLOCKS[r][-1] == 1]
    takers = [r for r in range(len(cores)) if BLOCKS[r][0] == 2]
    h_src = {d: [s for s in holders if topo.may_write(cores[s], cores[d])][0] for d in takers}
    h_to = [d for d in takers if h_src[d] == rank]

    xof = {}
    for bi, b in enumerate(blocks):
        own = b == rank
        for i, (lo, hi, eng) in enumerate(_pieces(b)):
            for s in range(lo, hi):
                xof[S * bi + s] = (T.xs if own else T.xr, s, sem[("lx%d" if own else "rx%d") % i],
                                   16 if own else eng[1], (bi, i), own or not first)

    def psum(j, c):
        return T["ps%d" % (NC * (j % AHEAD) + c)][:, 0:HB]

    def xcols(j, c):
        return xof[j][0][:, xof[j][1] * B + c * HB: xof[j][1] * B + (c + 1) * HB]

    def hcols(j, c):
        return T.ys[:, j * B + c * HB: j * B + (c + 1) * HB]

    def x_ready(q, j, seen):
        if xof[j][4] not in seen:
            seen.add(xof[j][4])
            q.wait_ge(xof[j][2], xof[j][3])

    msem = [sem["m%d" % c] for c in range(NC)]
    tsem = [sem["t%d" % c] for c in range(NC)]

    def done(q, n, parts=(0, NC)):
        for c in range(parts[0], parts[1]):
            q.wait_ge(tsem[c], n)

    mine = _pieces(rank)
    for i, (lo, hi, eng) in enumerate(mine):
        g.sync.dma_start(T.xs[:, lo * B:hi * B], T.x[:, lo * B:hi * B]).then_inc(sem["lx%d" % i], 16)
    g.scalar.dma_start(T.a_sb[:], T.a[:]).then_inc(sem.la, 16)
    g.vector.memset(T.ident[:], 1.0).then_inc(sem.ones, 1)
    g.wait_ge(sem.ones, 1)
    g.affine_select(T.ident[:], T.ident[:], [[-1, 128]], AluOpType.is_equal, 0.0, 0, 1).then_inc(sem.id, 1)

    tq, seen, put = g.tensor, set(), set()

    def prepare(upto, must):
        for k in range(jp, min(upto, nj - 1) + 1):
            if k not in put and (k == must or xof[k][5] or xof[k][4] in seen):
                x_ready(tq, k, seen)
                put.add(k)
                for c in range(NC):
                    tq.matmul(psum(k, c), T.ident[:], xcols(k, c), True, False)

    tq.wait_ge(sem.id, 1)
    prepare(jp + AHEAD - 1, jp)
    tq.wait_ge(sem.la, 16)
    for j in range(jp, nj):
        for c in range(NC):
            if j > 0:
                tq.wait_ge(tsem[c], j)
            else:
                for i, (lo, hi) in enumerate(H_PARTS):
                    if c == lo:
                        tq.wait_ge(sem["rh%d" % i], H_ENG[1])
            prev = hcols(j - 1, c) if j > 0 else T.hin[:, c * HB:(c + 1) * HB]
            tq.matmul(psum(j, c), T.a_sb[:], prev, False, True).then_inc(msem[c], 1)
        prepare(j + AHEAD - 1, j + 1)

    sq = g.scalar
    for j in range(nj):
        for c in range(NC):
            if j < jp:
                if c == 0:
                    sq.wait_ge(xof[j][2], xof[j][3])
                src = xcols(j, c)
            else:
                sq.wait_ge(msem[c], j - jp + 1)
                src = psum(j, c)
            sq.activation(hcols(j, c), src, ActivationFunctionType.Tanh).then_inc(tsem[c], 1)

    sent = 0
    if X_TO[rank] is not None:
        dst = cores[X_TO[rank]]
        rid, pid = topo.addr(dst, core)
        for i, (lo, hi, eng) in enumerate(mine):
            g.wait_ge(sem["lx%d" % i], 16)
            g.remote_dma(out_ap=T.xr[:, lo * B:hi * B], in_ap=T.xs[:, lo * B:hi * B], remote_sem=sem["rx%d" % i],
                         local_sem=sem.sx, pid=pid, routing_id=rid, dma_engine_mask=_sub(topo.mask(core, dst), eng))
            sent += eng[1]
    hsent = 0
    for d in h_to:
        dst = cores[d]
        rid, pid = topo.addr(dst, core)
        for i, (lo, hi) in enumerate(H_PARTS):
            done(g, nj, (lo, hi))
            g.remote_dma(out_ap=T.hin[:, lo * HB:hi * HB], in_ap=T.ys[:, (nj - 1) * B + lo * HB:(nj - 1) * B + hi * HB],
                         remote_sem=sem["rh%d" % i], local_sem=sem.sh, pid=pid, routing_id=rid,
                         dma_engine_mask=_sub(topo.mask(core, dst), H_ENG))
            hsent += H_ENG[1]
    if sent:
        g.wait_ge(sem.sx, sent)
    if hsent:
        g.wait_ge(sem.sh, hsent)

    if hsent:
        g.sync.wait_ge(sem.sh, hsent)
        parts = WHOLE
    else:
        parts = TAIL
    for part in parts:
        lo, hi = part[0], part[1]
        done(g.sync, j0 + hi)
        g.sync.dma_start(T.y[:, lo * B:hi * B], T.ys[:, (j0 + lo) * B:(j0 + hi) * B]).then_inc(sem.st, 16)
    g.sync.wait_ge(sem.st, 16 * len(parts))
